import numpy as np
import ml_dtypes


def mxq(x, axis, fmt="e4m3"):
    dtype, down = {"e4m3": (ml_dtypes.float8_e4m3fn, 7), "e5m2": (ml_dtypes.float8_e5m2, 14)}[fmt]
    v = np.moveaxis(np.asarray(x, np.float32).astype(ml_dtypes.bfloat16).astype(np.float64), axis, -1)
    blocks = v.reshape(v.shape[:-1] + (-1, 32))
    amax = np.abs(blocks).max(-1, keepdims=True)
    byte = np.maximum(np.where(amax > 0, np.frexp(amax)[1] - 1 + 127, 0) - down, 1)
    scale = np.exp2(byte - 127.0)
    codes = (blocks / scale).astype(np.float32).astype(dtype).astype(np.float64)
    return np.moveaxis((codes * scale).reshape(v.shape), -1, axis)


WIDE = False


def mx_kscale(k):
    if not WIDE:
        return np.ones(k)
    levels = np.array([10, -10, 5, -5, 0])
    if k % 512:
        return np.exp2(np.random.permutation(np.resize(levels, k // 32))).repeat(32)
    a = np.empty((k // 512, 16))
    for p in range(k // 512):
        a[p, :8] = np.random.permutation(np.resize(levels, 8))
        for g in range(8):
            far = levels[np.abs(levels - a[p, g]) >= 10]
            a[p, g + 8] = far[np.random.randint(len(far))]
    return np.exp2(a.ravel()).repeat(32)


def f64(x):
    return np.asarray(x).astype(np.float64)


def striped(idx):
    return np.tile(idx.reshape(-1, 16).T, (8, 1)).astype(np.uint16)


def unstriped(offs):
    return offs[:16].T.reshape(-1).astype(np.int64)


E2M1 = np.array([0.0, 0.5, 1.0, 1.5, 2.0, 3.0, 4.0, 6.0, -0.0, -0.5, -1.0, -1.5, -2.0, -3.0, -4.0, -6.0])


def pack_weight(w, fmt):
    k, n = w.shape
    w = f64(np.asarray(w, np.float32).astype(ml_dtypes.bfloat16)).reshape(k // 32, 32, n)
    amax = np.abs(w).max(1)
    if fmt == "e4m3":
        byte = np.frexp(amax)[1] - 1 + 127 - 7
    else:
        mant, ex = np.frexp(amax / 6.0)
        byte = np.where(mant > 0.5, ex, ex - 1) + 127
    byte = np.clip(np.where(amax > 0, byte, 1), 1, 254)
    scaled = (w * np.exp2(127.0 - byte)[:, None, :]).reshape(k, n).astype(np.float32)
    by_word = np.ascontiguousarray(scaled.reshape(k // 512, 128, 4, n).transpose(0, 1, 3, 2))
    if fmt == "e4m3":
        words = by_word.astype(ml_dtypes.float8_e4m3fn).view(np.uint8)
    else:
        c = by_word.astype(ml_dtypes.float4_e2m1fn).view(np.uint8) & 0xF
        words = (c[..., 0::2] | (c[..., 1::2] << 4)).reshape(k // 512, 128, 2 * n)
    return np.ascontiguousarray(words), np.ascontiguousarray(byte.astype(np.uint8).reshape(k // 512, 16, n))


def unpack_weight(words, scales, fmt):
    g, _, n = scales.shape
    words = np.ascontiguousarray(words).reshape(g, 128, n, -1)
    if fmt == "e4m3":
        vals = words.view(ml_dtypes.float8_e4m3fn).astype(np.float64)
    else:
        nib = np.empty((g, 128, n, 4), np.uint8)
        nib[..., 0::2] = words & 0xF
        nib[..., 1::2] = words >> 4
        vals = E2M1[nib]
    vals = vals * np.repeat(np.exp2(scales.astype(np.float64) - 127.0), 8, axis=1)[..., None]
    return vals.transpose(0, 1, 3, 2).reshape(g * 512, n)


def gelu(v):
    return 0.5 * v * (1.0 + np.tanh(np.sqrt(2.0 / np.pi) * (v + 0.044715 * v**3)))


K, H, T, S, P = 512, 1024, 4096, 1024, 512

def setup_inputs():
    n = np.random.standard_normal
    s = mx_kscale(K)[:, None]
    u = mx_kscale(H)[:, None]
    tab_words, tab_scales = pack_weight(n((K, T)) * s, "e4m3")
    w4_words, w4_scales = pack_weight(n((K, H)) / np.sqrt(K) / s * u.T, "e2m1")
    return {
        "tab_words": tab_words,
        "tab_scales": tab_scales,
        "offs": striped(np.random.permutation(T)[:S]),
        "pos1": striped(np.random.permutation(S)[:P]),
        "pos2": striped(np.random.permutation(S)[:P]),
        "w1": (n((K, H)) / np.sqrt(K) / s * u.T).astype(np.float32),
        "w4_words": w4_words,
        "w4_scales": w4_scales,
        "w3": (1.5 * n((K, H)) / np.sqrt(K) / s).astype(np.float32),
        "gain": (1.5 * np.exp(0.4 * n(H)) / np.sqrt(H) / u[:, 0] ** 2).astype(np.float32),
        "ctype": np.exp(0.5 * n((P, P))).astype(np.float32),
        "rowv": (0.6 * n(P)).astype(np.float32),
    }

def reference(tab_words, tab_scales, offs, pos1, pos2, w1, w4_words, w4_scales, w3, gain, ctype, rowv):
    v = unpack_weight(tab_words, tab_scales, "e4m3")[:, unstriped(offs)]
    w4 = unpack_weight(w4_words, w4_scales, "e2m1")
    ra = mxq(f64(w1), 0, "e4m3").T @ v
    rb = w4.T @ v
    st = mxq(f64(w3), 0, "e4m3").T @ v
    h = np.maximum(ra, rb) * np.tanh(st)
    x1 = h[:, unstriped(pos1)]
    x2 = np.abs(h[:, unstriped(pos2)]) * f64(gain)[:, None]
    e = mxq(x1, 0, "e4m3").T @ mxq(x2, 0, "e4m3")
    return e * f64(ctype) + f64(rowv)[None, :]

@@ -1,0 +1,262 @@
+from contextlib import ExitStack
+
+import concourse.mybir as mybir
+from concourse.masks import make_identity
+
+K, H, T, S, NP = 512, 1024, 4096, 1024, 512
+FLOPS = 2 * 3 * K * H * S + 2 * H * NP * NP
+
+F32 = mybir.dt.float32
+BF16 = mybir.dt.bfloat16
+I32 = mybir.dt.int32
+U32 = mybir.dt.uint32
+U16 = mybir.dt.uint16
+U8 = mybir.dt.uint8
+FP8X4 = mybir.dt.float8_e4m3fn_x4
+FP4X4 = mybir.dt.float4_e2m1fn_x4
+ACT = mybir.ActivationFunctionType
+ALU = mybir.AluOpType
+
+P = 128
+PACK = 4
+HALF = 512
+PASSES = H // 512
+TILES = PASSES * PACK
+
+
+def tile_list_lease_conflict_desk_kernel(
+    tc, tab_words, tab_scales, offs, pos1, pos2, w1, w4_words, w4_scales, w3, gain, ctype, rowv, out
+):
+    nc = tc.nc
+    with ExitStack() as ctx:
+        keep = ctx.enter_context(tc.tile_pool(name="keep", bufs=1))
+        ring = ctx.enter_context(tc.tile_pool(name="ring", bufs=2))
+        psum = ctx.enter_context(tc.psum_pool(name="psum", bufs=1))
+
+        offs_t = keep.tile([P, S // 16], U16, name="offs_t")
+        pos1_t = keep.tile([P, NP // 16], U16, name="pos1_t")
+        pos2_t = keep.tile([P, NP // 16], U16, name="pos2_t")
+        tabw = keep.tile([P, T], I32, name="tabw", align_bytes=64)
+        tabs = keep.tile([P, T], U8, name="tabs", align_bytes=64)
+        w4raw = keep.tile([P, 2 * H], U8, name="w4raw", align_bytes=64)
+        w4sraw = keep.tile([P, H], U8, name="w4sraw", align_bytes=64)
+        grow = keep.tile([P, P], F32, name="grow")
+        ident = keep.tile([P, P], F32, name="ident")
+
+        nc.gpsimd.memset(grow[:], 0.0)
+        nc.vector.memset(w4sraw[:].bitcast(I32), 0)
+        nc.vector.memset(tabs[:].bitcast(I32), 0)
+
+        nc.sync.dma_start(offs_t[:], offs)
+        nc.sync.dma_start(tabw[:], tab_words[0].rearrange("p t i -> p (t i)").bitcast(I32))
+        for q in range(4):
+            nc.scalar.dma_start(w4sraw[32 * q : 32 * q + 4, :].bitcast(I32), w4_scales[0, 4 * q : 4 * q + 4, :].bitcast(I32))
+        for b in range(PASSES):
+            nc.scalar.dma_start(
+                grow[PACK * b : PACK * (b + 1), :].rearrange("t (q i) -> t q i", i=8),
+                gain[512 * b : 512 * (b + 1)].rearrange("(q t i) -> t q i", t=PACK, i=8),
+            )
+        for q in range(4):
+            nc.sync.dma_start(tabs[32 * q : 32 * q + 4, :].bitcast(I32), tab_scales[0, 4 * q : 4 * q + 4, :].bitcast(I32))
+        make_identity(nc, ident[:])
+        nc.sync.dma_start(w4raw[:].bitcast(I32), w4_words[0].bitcast(I32))
+
+        wraw = {}
+
+        def load_w(b):
+            for name, w in (("w3", w3), ("w1", w1)):
+                wraw[name, b] = keep.tile([P, PACK, 512], F32, name="%sraw%d" % (name, b))
+                nc.sync.dma_start(wraw[name, b][:], w[:, 512 * b : 512 * (b + 1)].rearrange("(p j) c -> p j c", j=PACK))
+
+        load_w(0)
+        nc.sync.dma_start(pos2_t[:], pos2)
+        nc.sync.dma_start(pos1_t[:], pos1)
+        load_w(1)
+        ct = keep.tile([P, PACK, NP], F32, name="ct")
+        nc.sync.dma_start(ct[:], ctype.rearrange("(a p) j -> p a j", p=P))
+        rv = keep.tile([P, NP], F32, name="rv")
+        nc.sync.dma_start(rv[:], rowv.partition_broadcast(P))
+
+        gps = psum.tile([P, HALF], F32, name="gps", tag="st", bufs=3)
+        nc.tensor.transpose(gps[:, 0:P], grow[:], ident[:])
+        gcol = keep.tile([P, TILES], F32, name="gcol")
+        gpos = keep.tile([P, TILES], F32, name="gpos")
+        gsign = keep.tile([P, TILES], F32, name="gsign")
+        nc.vector.tensor_copy(gcol[:], gps[:, 0:TILES])
+        nc.vector.tensor_scalar(gpos[:], gcol[:], 0.0, 2.0, ALU.is_ge, ALU.mult)
+        nc.vector.tensor_scalar(gsign[:], gpos[:], 1.0, -1.0, ALU.mult, ALU.add)
+
+        vw = []
+        vs = []
+        for hf in range(2):
+            cols = offs_t[:, 32 * hf : 32 * (hf + 1)]
+            vw.append(keep.tile([P, HALF], U32, name="vw%d" % hf, align_bytes=64))
+            vs.append(keep.tile([P, HALF], U8, name="vs%d" % hf, align_bytes=64))
+            nc.vector.tensor_copy(vw[hf][:], tabw[:].bitcast(U32).indirect(cols))
+            nc.vector.tensor_copy(vs[hf][:], tabs[:].indirect(cols))
+
+        w4c = keep.tile([P, 2 * H], U8, name="w4c", align_bytes=64)
+        w4s = keep.tile([P, H], U8, name="w4s", align_bytes=64)
+        nc.vector.tensor_copy(
+            w4c[:].bitcast(I32).rearrange("p (b t q i) -> p b t q i", b=PASSES, t=PACK, i=4),
+            w4raw[:].bitcast(I32).rearrange("p (b q t i) -> p b t q i", b=PASSES, t=PACK, i=4),
+        )
+        nc.vector.tensor_copy(
+            w4s[:].bitcast(I32).rearrange("p (b t q i) -> p b t q i", b=PASSES, t=PACK, i=2),
+            w4sraw[:].bitcast(I32).rearrange("p (b q t i) -> p b t q i", b=PASSES, t=PACK, i=2),
+        )
+
+        wg = [keep.tile([P, 2, 512], BF16, name="wg%d" % u, align_bytes=64) for u in range(TILES)]
+        wc = [keep.tile([P, 2 * P], U32, name="wc%d" % u, align_bytes=64) for u in range(TILES)]
+        ws = [keep.tile([P, 2 * P], U8, name="ws%d" % u, align_bytes=64) for u in range(TILES)]
+
+        def cast_w(u, which, on_vector):
+            b, t = divmod(u, PACK)
+            src = wraw[("w3", "w1")[which], b][:].rearrange("p j (q t c i) -> p t q c j i", t=PACK, c=2, i=4)[:, t]
+            dst = wg[u][:, which, :].rearrange("p (q c i j) -> p q c j i", c=2, i=4, j=PACK)
+            if on_vector:
+                nc.vector.tensor_copy(dst, src)
+            else:
+                nc.scalar.copy(dst, src)
+
+        def quant_w(u, lo, hi):
+            nc.vector.quantize_mx(
+                out=wc[u][:, lo * P : hi * P].bitcast(FP8X4),
+                scales=ws[u][:, lo * P : hi * P],
+                in_=wg[u][:, lo:hi, :].rearrange("p a n -> p (a n)"),
+            )
+
+        banks = {}
+
+        def mm(u, hf, kind):
+            if kind == "rb":
+                lhs = w4c[:, 2 * P * u : 2 * P * (u + 1)].bitcast(FP4X4)
+                lsc = w4s[:, P * u : P * (u + 1)]
+            else:
+                a = 0 if kind == "st" else 1
+                lhs = wc[u][:, a * P : (a + 1) * P].bitcast(FP8X4)
+                lsc = ws[u][:, a * P : (a + 1) * P]
+            bank = psum.tile([P, HALF], F32, name=kind, tag=kind, bufs=2 if kind == "rb" else 3)
+            nc.tensor.matmul_mx(out=bank[:], lhsT=lhs, lhsT_scale=lsc, rhs=vw[hf][:].bitcast(FP8X4), rhs_scale=vs[hf][:], start=True, stop=True)
+            banks[u, hf, kind] = bank
+
+        th = {}
+        rb = {}
+        mx = {}
+        h = {}
+
+        def first_stage(u):
+            th[u] = ring.tile([P, S], F32, name="th", tag="th")
+            for hf in range(2):
+                mm(u, hf, "rb")
+                mm(u, hf, "st")
+                mm(u, hf, "ra")
+                rb[u, hf] = ring.tile([P, HALF], F32, name="rbs", tag="rbs", bufs=4)
+                nc.scalar.copy(rb[u, hf][:], banks[u, hf, "rb"][:])
+                nc.scalar.activation(th[u][:, HALF * hf : HALF * (hf + 1)], banks[u, hf, "st"][:], ACT.Tanh, scale=gsign[:, u : u + 1])
+
+        def larger(u, hf):
+            if hf == 0:
+                mx[u] = ring.tile([P, S], F32, name="mx", tag="mx")
+            nc.vector.tensor_tensor(mx[u][:, HALF * hf : HALF * (hf + 1)], banks[u, hf, "ra"][:], rb[u, hf][:], ALU.max)
+
+        def product(u):
+            h[u] = ring.tile([P, S], F32, name="h", tag="h", bufs=3)
+            nc.vector.tensor_tensor(h[u][:], mx[u][:], th[u][:], ALU.mult)
+
+        x1p = [keep.tile([P, PACK, NP], BF16, name="x1p%d" % b) for b in range(PASSES)]
+        x2p = [keep.tile([P, PACK, NP], BF16, name="x2p%d" % b) for b in range(PASSES)]
+
+        def pick1(u):
+            b, t = divmod(u, PACK)
+            nc.vector.tensor_copy(x1p[b][:, t, :], h[u][:].indirect(pos1_t[:]))
+
+        def pick2(u):
+            b, t = divmod(u, PACK)
+            g2 = ring.tile([P, NP], F32, name="g2", tag="g2")
+            nc.vector.tensor_copy(g2[:], h[u][:].indirect(pos2_t[:]))
+            nc.scalar.activation(x2p[b][:, t, :], g2[:], ACT.Abs, scale=gcol[:, u : u + 1])
+
+        xg = {}
+        xc = {}
+        xs = {}
+
+        def weave(name, planes, b, pieces, on_vector):
+            xg[name, b] = keep.tile([P, PACK * NP], BF16, name="%sg%d" % (name, b), align_bytes=64)
+            n = NP // pieces
+            for a in range(pieces):
+                src = planes[:, :, n * a : n * (a + 1)].rearrange("p t (c i) -> p c t i", i=4)
+                dst = xg[name, b][:, PACK * n * a : PACK * n * (a + 1)].rearrange("p (c i t) -> p c t i", i=4, t=PACK)
+                if on_vector:
+                    nc.vector.tensor_copy(dst, src)
+                else:
+                    nc.scalar.copy(dst, src)
+
+        def quant_x(name, b):
+            xc[name, b] = keep.tile([P, NP], U32, name="%sc%d" % (name, b), align_bytes=64)
+            xs[name, b] = keep.tile([P, NP], U8, name="%ss%d" % (name, b), align_bytes=64)
+            nc.vector.quantize_mx(out=xc[name, b][:].bitcast(FP8X4), scales=xs[name, b][:], in_=xg[name, b][:])
+
+        cast_w(0, 0, False)
+        quant_w(0, 0, 1)
+        cast_w(0, 1, True)
+        cast_w(1, 0, False)
+        quant_w(0, 1, 2)
+        first_stage(0)
+        cast_w(1, 1, False)
+        quant_w(1, 0, 2)
+        for u in range(TILES):
+            if u + 2 < TILES:
+                cast_w(u + 2, 0, False)
+                cast_w(u + 2, 1, False)
+            larger(u, 0)
+            larger(u, 1)
+            if u + 1 < TILES:
+                first_stage(u + 1)
+            if u + 2 < TILES:
+                quant_w(u + 2, 0, 2)
+            if u > 0:
+                pick2(u - 1)
+            product(u)
+            if u > 0:
+                pick1(u - 1)
+            if u == PACK:
+                weave("x1", x1p[0], 0, 4, False)
+                weave("x2", x2p[0], 0, 4, False)
+        last = TILES - 1
+        quant_x("x1", 0)
+        pick2(last)
+        pick1(last)
+        weave("x2", x2p[1], 1, 2, False)
+        weave("x1", x1p[1], 1, 1, True)
+        quant_x("x2", 0)
+        quant_x("x1", 1)
+        quant_x("x2", 1)
+
+        es = []
+        for a in range(PACK):
+            e = psum.tile([P, NP], F32, name="e", tag="st" if a % 2 else "ra", bufs=3)
+            for b in range(PASSES):
+                nc.tensor.matmul_mx(
+                    out=e[:],
+                    lhsT=xc["x1", b][:, P * a : P * (a + 1)].bitcast(FP8X4),
+                    lhsT_scale=xs["x1", b][:, P * a : P * (a + 1)],
+                    rhs=xc["x2", b][:].bitcast(FP8X4),
+                    rhs_scale=xs["x2", b][:],
+                    start=(b == 0),
+                    stop=(b == PASSES - 1),
+                )
+            es.append(e)
+        scaled = []
+
+        def finish(a):
+            res = keep.tile([P, NP], F32, name="res%d" % a)
+            nc.vector.tensor_tensor(res[:], scaled[a][:], rv[:], ALU.add)
+            nc.sync.dma_start(out[P * a : P * (a + 1), :], res[:])
+
+        for a in range(PACK):
+            scaled.append(keep.tile([P, NP], F32, name="scaled%d" % a))
+            nc.vector.tensor_tensor(scaled[a][:], es[a][:], ct[:, a, :], ALU.mult)
+            if a > 0:
+                finish(a - 1)
+        finish(PACK - 1)

@@ -36,206 +36,231 @@ def tile_list_lease_conflict_desk_kernel(
         offs_t = keep.tile([P, S // 16], U16, name="offs_t")
         pos1_t = keep.tile([P, NP // 16], U16, name="pos1_t")
         pos2_t = keep.tile([P, NP // 16], U16, name="pos2_t")
-        tabw = keep.tile([P, T], I32, name="tabw", align_bytes=64)
+        tabw = keep.tile([P, T], I32, name="tabw", tag="table", align_bytes=64)
+        tabs_in = keep.tile([16, T // 4], I32, name="tabs_in", align_bytes=64)
         tabs = keep.tile([P, T], U8, name="tabs", align_bytes=64)
         w4raw = keep.tile([P, 2 * H], U8, name="w4raw", align_bytes=64)
-        w4sraw = keep.tile([P, H], U8, name="w4sraw", align_bytes=64)
-        grow = keep.tile([P, P], F32, name="grow")
+        w4sraw = keep.tile([16, H // 4], I32, name="w4sraw", align_bytes=64)
+        gain_in = keep.tile([PACK, PASSES * P], F32, name="gain_in")
+        grow = keep.tile([P, PASSES * P], F32, name="grow")
         ident = keep.tile([P, P], F32, name="ident")
-
-        nc.gpsimd.memset(grow[:], 0.0)
-        nc.vector.memset(w4sraw[:].bitcast(I32), 0)
-        nc.vector.memset(tabs[:].bitcast(I32), 0)
-
-        nc.sync.dma_start(offs_t[:], offs)
-        nc.sync.dma_start(tabw[:], tab_words[0].rearrange("p t i -> p (t i)").bitcast(I32))
-        for q in range(4):
-            nc.scalar.dma_start(w4sraw[32 * q : 32 * q + 4, :].bitcast(I32), w4_scales[0, 4 * q : 4 * q + 4, :].bitcast(I32))
-        for b in range(PASSES):
-            nc.scalar.dma_start(
-                grow[PACK * b : PACK * (b + 1), :].rearrange("t (q i) -> t q i", i=8),
-                gain[512 * b : 512 * (b + 1)].rearrange("(q t i) -> t q i", t=PACK, i=8),
-            )
-        for q in range(4):
-            nc.sync.dma_start(tabs[32 * q : 32 * q + 4, :].bitcast(I32), tab_scales[0, 4 * q : 4 * q + 4, :].bitcast(I32))
-        make_identity(nc, ident[:])
-        nc.sync.dma_start(w4raw[:].bitcast(I32), w4_words[0].bitcast(I32))
-
+        wsrc = {"w3": w3, "w1": w1}
         wraw = {}
 
-        def load_w(b):
-            for name, w in (("w3", w3), ("w1", w1)):
-                wraw[name, b] = keep.tile([P, PACK, 512], F32, name="%sraw%d" % (name, b))
-                nc.sync.dma_start(wraw[name, b][:], w[:, 512 * b : 512 * (b + 1)].rearrange("(p j) c -> p j c", j=PACK))
+        def load_w(name, b):
+            wraw[name, b] = keep.tile([P, PACK, 512], F32, name="%sraw%d" % (name, b), tag="table" if (name, b) == ("w1", 1) else name, align_bytes=64)
+            nc.sync.dma_start(wraw[name, b][:], wsrc[name][:, 512 * b : 512 * (b + 1)].rearrange("(p j) c -> p j c", j=PACK))
 
-        load_w(0)
+        nc.sync.dma_start(tabs_in[:], tab_scales[0].bitcast(I32))
+        nc.sync.dma_start(offs_t[:], offs)
+        nc.sync.dma_start(w4sraw[:], w4_scales[0].bitcast(I32))
+        nc.sync.dma_start(
+            gain_in[:].rearrange("t (g i) -> t g i", i=8),
+            gain.rearrange("(g t i) -> t g i", t=PACK, i=8),
+        )
+        nc.sync.dma_start(w4raw[:].bitcast(I32), w4_words[0].bitcast(I32))
+        load_w("w1", 0)
+        nc.sync.dma_start(tabw[:], tab_words[0].rearrange("p t i -> p (t i)").bitcast(I32))
         nc.sync.dma_start(pos2_t[:], pos2)
         nc.sync.dma_start(pos1_t[:], pos1)
-        load_w(1)
-        ct = keep.tile([P, PACK, NP], F32, name="ct")
-        nc.sync.dma_start(ct[:], ctype.rearrange("(a p) j -> p a j", p=P))
-        rv = keep.tile([P, NP], F32, name="rv")
-        nc.sync.dma_start(rv[:], rowv.partition_broadcast(P))
 
-        gps = psum.tile([P, HALF], F32, name="gps", tag="st", bufs=3)
-        nc.tensor.transpose(gps[:, 0:P], grow[:], ident[:])
+        nc.gpsimd.memset(grow[:], 0.0)
+        make_identity(nc, ident[:])
+        nc.vector.memset(tabs[:].bitcast(I32), 0)
+        warm = keep.tile([P, 1], F32, name="warm")
+        nc.scalar.activation(warm[:], ident[:, 0:1], ACT.Tanh)
+        nc.vector.tensor_copy(tabs[0:16, :].bitcast(I32), tabs_in[:])
+
+        nc.scalar.copy(grow[0:PACK, :], gain_in[:])
+        gps = psum.tile([P, HALF], F32, name="gps", tag="spare0")
+        for b in range(PASSES):
+            nc.tensor.transpose(gps[:, P * b : P * (b + 1)], grow[:, P * b : P * (b + 1)], ident[:])
         gcol = keep.tile([P, TILES], F32, name="gcol")
         gpos = keep.tile([P, TILES], F32, name="gpos")
         gsign = keep.tile([P, TILES], F32, name="gsign")
-        nc.vector.tensor_copy(gcol[:], gps[:, 0:TILES])
-        nc.vector.tensor_scalar(gpos[:], gcol[:], 0.0, 2.0, ALU.is_ge, ALU.mult)
-        nc.vector.tensor_scalar(gsign[:], gpos[:], 1.0, -1.0, ALU.mult, ALU.add)
-
-        vw = []
-        vs = []
-        for hf in range(2):
-            cols = offs_t[:, 32 * hf : 32 * (hf + 1)]
-            vw.append(keep.tile([P, HALF], U32, name="vw%d" % hf, align_bytes=64))
-            vs.append(keep.tile([P, HALF], U8, name="vs%d" % hf, align_bytes=64))
-            nc.vector.tensor_copy(vw[hf][:], tabw[:].bitcast(U32).indirect(cols))
-            nc.vector.tensor_copy(vs[hf][:], tabs[:].indirect(cols))
-
+        nc.scalar.copy(gcol[:].rearrange("p (b t) -> p b t", t=PACK), gps[:, 0 : PASSES * P].rearrange("p (b c) -> p b c", b=PASSES)[:, :, 0:PACK])
+        nc.gpsimd.tensor_scalar(gpos[:], gcol[:], 0.0, 2.0, ALU.is_ge, ALU.mult)
+        nc.gpsimd.tensor_scalar(gsign[:], gpos[:], 1.0, -1.0, ALU.mult, ALU.add)
+        vw = [keep.tile([P, HALF], U32, name="vw%d" % hf, align_bytes=64) for hf in range(2)]
+        vsg = keep.tile([P, S], U8, name="vsg", tag="w3", align_bytes=64)
+        rows = keep.tile([16, (S + H) // 4], I32, name="rows", tag="rows", align_bytes=64)
+        planes = keep.tile([P, S + H], U8, name="planes", align_bytes=64)
         w4c = keep.tile([P, 2 * H], U8, name="w4c", align_bytes=64)
-        w4s = keep.tile([P, H], U8, name="w4s", align_bytes=64)
+        nc.vector.tensor_copy(
+            rows[:, S // 4 :].rearrange("p (b t q i) -> p b t q i", b=PASSES, t=PACK, i=2),
+            w4sraw[:].rearrange("p (b q t i) -> p b t q i", b=PASSES, t=PACK, i=2),
+        )
+        nc.vector.tensor_copy(vsg[:], tabs[:].indirect(offs_t[:]))
         nc.vector.tensor_copy(
             w4c[:].bitcast(I32).rearrange("p (b t q i) -> p b t q i", b=PASSES, t=PACK, i=4),
             w4raw[:].bitcast(I32).rearrange("p (b q t i) -> p b t q i", b=PASSES, t=PACK, i=4),
         )
-        nc.vector.tensor_copy(
-            w4s[:].bitcast(I32).rearrange("p (b t q i) -> p b t q i", b=PASSES, t=PACK, i=2),
-            w4sraw[:].bitcast(I32).rearrange("p (b q t i) -> p b t q i", b=PASSES, t=PACK, i=2),
-        )
+        nc.vector.tensor_copy(rows[:, 0 : S // 4], vsg[0:16, :].bitcast(I32))
+        for q in range(4):
+            nc.sync.dma_start(planes[32 * q : 32 * q + 4, :].bitcast(I32), rows[4 * q : 4 * q + 4, :])
+        load_w("w3", 0)
+        rv = keep.tile([P, NP], F32, name="rv", tag="rows", align_bytes=64)
+        nc.sync.dma_start(rv[:], rowv.partition_broadcast(P))
 
-        wg = [keep.tile([P, 2, 512], BF16, name="wg%d" % u, align_bytes=64) for u in range(TILES)]
-        wc = [keep.tile([P, 2 * P], U32, name="wc%d" % u, align_bytes=64) for u in range(TILES)]
-        ws = [keep.tile([P, 2 * P], U8, name="ws%d" % u, align_bytes=64) for u in range(TILES)]
+        groups = [[("w1", u) for u in range(PACK)], [("w3", 0)], [("w3", 1)], [("w3", 2), ("w3", 3)]]
+        groups.extend([("w3", u), ("w1", u)] for u in range(PACK, TILES))
+        wg = [keep.tile([P, 512 * len(g)], BF16, name="wg%d" % n, align_bytes=64) for n, g in enumerate(groups)]
+        wcs = [keep.tile([P, P * len(g)], U32, name="wc%d" % n, align_bytes=64) for n, g in enumerate(groups)]
+        wss = [keep.tile([P, P * len(g)], U8, name="ws%d" % n, align_bytes=64) for n, g in enumerate(groups)]
+        place = {key: (n, a) for n, g in enumerate(groups) for a, key in enumerate(g)}
 
-        def cast_w(u, which, on_vector):
-            b, t = divmod(u, PACK)
-            src = wraw[("w3", "w1")[which], b][:].rearrange("p j (q t c i) -> p t q c j i", t=PACK, c=2, i=4)[:, t]
-            dst = wg[u][:, which, :].rearrange("p (q c i j) -> p q c j i", c=2, i=4, j=PACK)
-            if on_vector:
-                nc.vector.tensor_copy(dst, src)
-            else:
-                nc.scalar.copy(dst, src)
-
-        def quant_w(u, lo, hi):
-            nc.vector.quantize_mx(
-                out=wc[u][:, lo * P : hi * P].bitcast(FP8X4),
-                scales=ws[u][:, lo * P : hi * P],
-                in_=wg[u][:, lo:hi, :].rearrange("p a n -> p (a n)"),
-            )
-
-        banks = {}
-
-        def mm(u, hf, kind):
-            if kind == "rb":
-                lhs = w4c[:, 2 * P * u : 2 * P * (u + 1)].bitcast(FP4X4)
-                lsc = w4s[:, P * u : P * (u + 1)]
-            else:
-                a = 0 if kind == "st" else 1
-                lhs = wc[u][:, a * P : (a + 1) * P].bitcast(FP8X4)
-                lsc = ws[u][:, a * P : (a + 1) * P]
-            bank = psum.tile([P, HALF], F32, name=kind, tag=kind, bufs=2 if kind == "rb" else 3)
-            nc.tensor.matmul_mx(out=bank[:], lhsT=lhs, lhsT_scale=lsc, rhs=vw[hf][:].bitcast(FP8X4), rhs_scale=vs[hf][:], start=True, stop=True)
-            banks[u, hf, kind] = bank
-
-        th = {}
-        rb = {}
-        mx = {}
-        h = {}
-
-        def first_stage(u):
-            th[u] = ring.tile([P, S], F32, name="th", tag="th")
-            for hf in range(2):
-                mm(u, hf, "rb")
-                mm(u, hf, "st")
-                mm(u, hf, "ra")
-                rb[u, hf] = ring.tile([P, HALF], F32, name="rbs", tag="rbs", bufs=4)
-                nc.scalar.copy(rb[u, hf][:], banks[u, hf, "rb"][:])
-                nc.scalar.activation(th[u][:, HALF * hf : HALF * (hf + 1)], banks[u, hf, "st"][:], ACT.Tanh, scale=gsign[:, u : u + 1])
-
-        def larger(u, hf):
-            if hf == 0:
-                mx[u] = ring.tile([P, S], F32, name="mx", tag="mx")
-            nc.vector.tensor_tensor(mx[u][:, HALF * hf : HALF * (hf + 1)], banks[u, hf, "ra"][:], rb[u, hf][:], ALU.max)
-
-        def product(u):
-            h[u] = ring.tile([P, S], F32, name="h", tag="h", bufs=3)
-            nc.vector.tensor_tensor(h[u][:], mx[u][:], th[u][:], ALU.mult)
-
-        x1p = [keep.tile([P, PACK, NP], BF16, name="x1p%d" % b) for b in range(PASSES)]
-        x2p = [keep.tile([P, PACK, NP], BF16, name="x2p%d" % b) for b in range(PASSES)]
-
-        def pick1(u):
-            b, t = divmod(u, PACK)
-            nc.vector.tensor_copy(x1p[b][:, t, :], h[u][:].indirect(pos1_t[:]))
-
-        def pick2(u):
-            b, t = divmod(u, PACK)
-            g2 = ring.tile([P, NP], F32, name="g2", tag="g2")
-            nc.vector.tensor_copy(g2[:], h[u][:].indirect(pos2_t[:]))
-            nc.scalar.activation(x2p[b][:, t, :], g2[:], ACT.Abs, scale=gcol[:, u : u + 1])
-
-        xg = {}
-        xc = {}
-        xs = {}
-
-        def weave(name, planes, b, pieces, on_vector):
-            xg[name, b] = keep.tile([P, PACK * NP], BF16, name="%sg%d" % (name, b), align_bytes=64)
-            n = NP // pieces
-            for a in range(pieces):
-                src = planes[:, :, n * a : n * (a + 1)].rearrange("p t (c i) -> p c t i", i=4)
-                dst = xg[name, b][:, PACK * n * a : PACK * n * (a + 1)].rearrange("p (c i t) -> p c t i", i=4, t=PACK)
+        def cast_group(n, on_vector=False):
+            for a, (name, u) in enumerate(groups[n]):
+                b, t = divmod(u, PACK)
+                src = wraw[name, b][:].rearrange("p j (q t c i) -> p t q c j i", t=PACK, c=2, i=4)[:, t]
+                dst = wg[n][:, 512 * a : 512 * (a + 1)].rearrange("p (q c i j) -> p q c j i", c=2, i=4, j=PACK)
                 if on_vector:
                     nc.vector.tensor_copy(dst, src)
                 else:
                     nc.scalar.copy(dst, src)
 
-        def quant_x(name, b):
-            xc[name, b] = keep.tile([P, NP], U32, name="%sc%d" % (name, b), align_bytes=64)
-            xs[name, b] = keep.tile([P, NP], U8, name="%ss%d" % (name, b), align_bytes=64)
-            nc.vector.quantize_mx(out=xc[name, b][:].bitcast(FP8X4), scales=xs[name, b][:], in_=xg[name, b][:])
+        def quant_group(n):
+            nc.vector.quantize_mx(out=wcs[n][:].bitcast(FP8X4), scales=wss[n][:], in_=wg[n][:])
 
-        cast_w(0, 0, False)
-        quant_w(0, 0, 1)
-        cast_w(0, 1, True)
-        cast_w(1, 0, False)
-        quant_w(0, 1, 2)
+        cast_group(0)
+        quant_group(0)
+
+        nc.vector.tensor_copy(vw[0][:], tabw[:].bitcast(U32).indirect(offs_t[:, 0:32]))
+        nc.vector.tensor_copy(vw[1][:], tabw[:].bitcast(U32).indirect(offs_t[:, 32:64]))
+        load_w("w1", 1)
+
+        def mm(u, hf, kind):
+            if kind == "rb":
+                lhs = w4c[:, 2 * P * u : 2 * P * (u + 1)].bitcast(FP4X4)
+                lsc = planes[:, S + P * u : S + P * (u + 1)]
+            else:
+                n, a = place["w3" if kind == "st" else "w1", u]
+                lhs = wcs[n][:, P * a : P * (a + 1)].bitcast(FP8X4)
+                lsc = wss[n][:, P * a : P * (a + 1)]
+            turn = (u + {"st": 0, "ra": 2, "rb": 1}[kind]) % 3
+            bank = psum.tile([P, HALF], F32, name=kind, tag="spare%d" % hf if (u, kind) == (1, "ra") else "turn%d%d" % (turn, hf))
+            nc.tensor.matmul_mx(out=bank[:], lhsT=lhs, lhsT_scale=lsc, rhs=vw[hf][:].bitcast(FP8X4), rhs_scale=planes[:, HALF * hf : HALF * (hf + 1)], start=True, stop=True)
+            return bank
+
+        x1p = [keep.tile([P, PACK, NP], F32, name="x1p%d" % b) for b in range(PASSES)]
+        g2p = [keep.tile([P, PACK, NP], F32, name="g2p%d" % b) for b in range(PASSES)]
+        x2p = [keep.tile([P, PACK, NP], BF16, name="x2p%d" % b) for b in range(PASSES)]
+        th = {}
+        ra = {}
+        mx = {}
+        h = {}
+
+        def rb_place(u, hf):
+            b, t = divmod(max(u - 1, 0), PACK)
+            return (g2p, x1p)[hf][b][:, t, :]
+
+        def first_stage(u):
+            th[u] = ring.tile([P, S], F32, name="th", tag="th")
+            for hf in range(2):
+                st = mm(u, hf, "st")
+                nc.scalar.activation(th[u][:, HALF * hf : HALF * (hf + 1)], st[:], ACT.Tanh, scale=gsign[:, u : u + 1])
+            for hf in range(2):
+                rb = mm(u, hf, "rb")
+                nc.scalar.copy(rb_place(u, hf), rb[:])
+                ra[u, hf] = mm(u, hf, "ra")
+
+        def larger(u):
+            mx[u] = ring.tile([P, S], F32, name="mx", tag="mx")
+            for hf in range(2):
+                nc.vector.tensor_tensor(mx[u][:, HALF * hf : HALF * (hf + 1)], ra[u, hf][:], rb_place(u, hf), ALU.max)
+
+        def product(u):
+            h[u] = ring.tile([P, S], F32, name="h", tag="h")
+            nc.vector.tensor_tensor(h[u][:], mx[u][:], th[u][:], ALU.mult)
+
+        def pick1(u, lo=0, hi=NP):
+            b, t = divmod(u, PACK)
+            nc.vector.tensor_copy(x1p[b][:, t, lo:hi], h[u][:].indirect(pos1_t[:, lo // 16 : hi // 16]))
+
+        def pick2(u, lo=0, hi=NP):
+            b, t = divmod(u, PACK)
+            nc.vector.tensor_copy(g2p[b][:, t, lo:hi], h[u][:].indirect(pos2_t[:, lo // 16 : hi // 16]))
+            nc.scalar.activation(x2p[b][:, t, lo:hi], g2p[b][:, t, lo:hi], ACT.Abs, scale=gcol[:, u : u + 1])
+
+        xg = {}
+        xc = {}
+        xs = {}
+        for name in ("x1", "x2"):
+            for b in range(PASSES):
+                xg[name, b] = keep.tile([P, PACK * NP], BF16, name="%sg%d" % (name, b), align_bytes=64)
+                xc[name, b] = keep.tile([P, NP], U32, name="%sc%d" % (name, b), align_bytes=64)
+                xs[name, b] = keep.tile([P, NP], U8, name="%ss%d" % (name, b), align_bytes=64)
+
+        def weave(name, b, lo, hi, on_vector=False):
+            src = {"x1": x1p, "x2": x2p}[name][b][:, :, lo:hi].rearrange("p t (c i) -> p c t i", i=4)
+            dst = xg[name, b][:, PACK * lo : PACK * hi].rearrange("p (c i t) -> p c t i", i=4, t=PACK)
+            if on_vector:
+                nc.vector.tensor_copy(dst, src)
+            else:
+                nc.scalar.copy(dst, src)
+
+        def weave_pair(name, t, lo, hi, on_vector=False):
+            src = {"x1": x1p, "x2": x2p}[name][1][:, t : t + 2, lo:hi].rearrange("p t c -> p c t")
+            dst = xg[name, 1][:, PACK * lo : PACK * hi].rearrange("p (c t) -> p c t", t=PACK)[:, :, t : t + 2]
+            if on_vector:
+                nc.vector.tensor_copy(dst, src)
+            else:
+                nc.scalar.copy(dst, src)
+
+        def quant_x(name, b, lo=0, hi=NP):
+            nc.vector.quantize_mx(
+                out=xc[name, b][:, lo:hi].bitcast(FP8X4), scales=xs[name, b][:, lo:hi], in_=xg[name, b][:, PACK * lo : PACK * hi]
+            )
+
+        cast_group(1, True)
+        cast_group(2, True)
+        ct = keep.tile([P, PACK, NP], F32, name="ct", tag="w1", align_bytes=64)
+        nc.sync.dma_start(ct[:], ctype.rearrange("(a p) j -> p a j", p=P))
+        quant_group(1)
+        quant_group(2)
         first_stage(0)
-        cast_w(1, 1, False)
-        quant_w(1, 0, 2)
         for u in range(TILES):
-            if u + 2 < TILES:
-                cast_w(u + 2, 0, False)
-                cast_w(u + 2, 1, False)
-            larger(u, 0)
-            larger(u, 1)
+            ahead = place.get(("w3", u + 2), (None, None))
+            larger(u)
             if u + 1 < TILES:
                 first_stage(u + 1)
-            if u + 2 < TILES:
-                quant_w(u + 2, 0, 2)
+            if ahead[1] is not None and u != 1:
+                cast_group(ahead[0], u == 0)
+            if u == 0:
+                load_w("w3", 1)
             if u > 0:
                 pick2(u - 1)
             product(u)
             if u > 0:
                 pick1(u - 1)
-            if u == PACK:
-                weave("x1", x1p[0], 0, 4, False)
-                weave("x2", x2p[0], 0, 4, False)
+            if ahead[1] is not None and u != 1:
+                quant_group(ahead[0])
+            if u in (PACK, PACK + 1):
+                name = "x2" if u == PACK else "x1"
+                for lo in range(0, NP, P):
+                    weave(name, 0, lo, lo + P)
+            if u == PACK + 2:
+                for name in ("x2", "x1"):
+                    for lo in (0, NP // 2):
+                        weave_pair(name, 0, lo, lo + NP // 2)
+            if u in (PACK + 2, PACK + 3):
+                quant_x("x2" if u == PACK + 2 else "x1", 0)
         last = TILES - 1
-        quant_x("x1", 0)
-        pick2(last)
-        pick1(last)
-        weave("x2", x2p[1], 1, 2, False)
-        weave("x1", x1p[1], 1, 1, True)
-        quant_x("x2", 0)
-        quant_x("x1", 1)
-        quant_x("x2", 1)
+        mid = NP // 2
+        for lo in (0, mid):
+            pick2(last, lo, lo + mid)
+            weave_pair("x2", 2, lo, lo + mid)
+        for lo in (0, mid):
+            pick1(last, lo, lo + mid)
+        for lo in (0, mid):
+            weave_pair("x1", 2, lo, lo + mid, True)
+        for name in ("x1", "x2"):
+            for lo in (0, mid):
+                quant_x(name, 1, lo, lo + mid)
 
         es = []
         for a in range(PACK):
-            e = psum.tile([P, NP], F32, name="e", tag="st" if a % 2 else "ra", bufs=3)
+            e = psum.tile([P, NP], F32, name="e", tag="turn%d%d" % ((TILES - 1 + a // 2) % 3, a % 2))
             for b in range(PASSES):
                 nc.tensor.matmul_mx(
                     out=e[:],
@@ -247,16 +272,13 @@ def tile_list_lease_conflict_desk_kernel(
                     stop=(b == PASSES - 1),
                 )
             es.append(e)
-        scaled = []
-
-        def finish(a):
-            res = keep.tile([P, NP], F32, name="res%d" % a)
-            nc.vector.tensor_tensor(res[:], scaled[a][:], rv[:], ALU.add)
-            nc.sync.dma_start(out[P * a : P * (a + 1), :], res[:])
-
+        scaled = [keep.tile([P, NP], F32, name="scaled%d" % a) for a in range(PACK)]
+        res = [keep.tile([P, NP], F32, name="res%d" % a) for a in range(PACK)]
         for a in range(PACK):
-            scaled.append(keep.tile([P, NP], F32, name="scaled%d" % a))
             nc.vector.tensor_tensor(scaled[a][:], es[a][:], ct[:, a, :], ALU.mult)
-            if a > 0:
-                finish(a - 1)
-        finish(PACK - 1)
+        for a in range(PACK):
+            adder = nc.gpsimd if a == 0 else nc.vector
+            step = mid if a == PACK - 1 else NP
+            for lo in range(0, NP, step):
+                adder.tensor_tensor(res[a][:, lo : lo + step], scaled[a][:, lo : lo + step], rv[:, lo : lo + step], ALU.add)
+                nc.sync.dma_start(out[P * a : P * (a + 1), lo : lo + step], res[a][:, lo : lo + step])

@@ -19,9 +19,14 @@ ALU = mybir.AluOpType
 
 P = 128
 PACK = 4
+PASS = P * PACK
+BLOCKS = PASS // 32
+RUN = 8
 HALF = 512
-PASSES = H // 512
+PASSES = H // PASS
 TILES = PASSES * PACK
+OUT_TILES = NP // P
+MID = NP // 2
 
 
 def tile_list_lease_conflict_desk_kernel(
@@ -37,31 +42,31 @@ def tile_list_lease_conflict_desk_kernel(
         pos1_t = keep.tile([P, NP // 16], U16, name="pos1_t")
         pos2_t = keep.tile([P, NP // 16], U16, name="pos2_t")
         tabw = keep.tile([P, T], I32, name="tabw", tag="table", align_bytes=64)
-        tabs_in = keep.tile([16, T // 4], I32, name="tabs_in", align_bytes=64)
+        tabs_in = keep.tile([BLOCKS, T // 4], I32, name="tabs_in", align_bytes=64)
         tabs = keep.tile([P, T], U8, name="tabs", align_bytes=64)
         w4raw = keep.tile([P, 2 * H], U8, name="w4raw", align_bytes=64)
-        w4sraw = keep.tile([16, H // 4], I32, name="w4sraw", align_bytes=64)
+        w4sraw = keep.tile([BLOCKS, H // 4], I32, name="w4sraw", align_bytes=64)
         gain_in = keep.tile([PACK, PASSES * P], F32, name="gain_in")
         grow = keep.tile([P, PASSES * P], F32, name="grow")
         ident = keep.tile([P, P], F32, name="ident")
         wsrc = {"w3": w3, "w1": w1}
         wraw = {}
 
-        def load_w(name, b):
-            wraw[name, b] = keep.tile([P, PACK, 512], F32, name="%sraw%d" % (name, b), tag="table" if (name, b) == ("w1", 1) else name, align_bytes=64)
-            nc.sync.dma_start(wraw[name, b][:], wsrc[name][:, 512 * b : 512 * (b + 1)].rearrange("(p j) c -> p j c", j=PACK))
+        def load_w(name, b, tag):
+            wraw[name, b] = keep.tile([P, PACK, PASS], F32, name="%sraw%d" % (name, b), tag=tag, align_bytes=64)
+            nc.sync.dma_start(wraw[name, b][:], wsrc[name][:, PASS * b : PASS * (b + 1)].rearrange("(p j) c -> p j c", j=PACK))
 
         nc.sync.dma_start(tabs_in[:], tab_scales[0].bitcast(I32))
         nc.sync.dma_start(offs_t[:], offs)
+        nc.sync.dma_start(pos2_t[:], pos2)
         nc.sync.dma_start(w4sraw[:], w4_scales[0].bitcast(I32))
         nc.sync.dma_start(
-            gain_in[:].rearrange("t (g i) -> t g i", i=8),
-            gain.rearrange("(g t i) -> t g i", t=PACK, i=8),
+            gain_in[:].rearrange("t (g i) -> t g i", i=RUN),
+            gain.rearrange("(g t i) -> t g i", t=PACK, i=RUN),
         )
         nc.sync.dma_start(w4raw[:].bitcast(I32), w4_words[0].bitcast(I32))
-        load_w("w1", 0)
         nc.sync.dma_start(tabw[:], tab_words[0].rearrange("p t i -> p (t i)").bitcast(I32))
-        nc.sync.dma_start(pos2_t[:], pos2)
+        load_w("w1", 0, "w1")
         nc.sync.dma_start(pos1_t[:], pos1)
 
         nc.gpsimd.memset(grow[:], 0.0)
@@ -69,67 +74,73 @@ def tile_list_lease_conflict_desk_kernel(
         nc.vector.memset(tabs[:].bitcast(I32), 0)
         warm = keep.tile([P, 1], F32, name="warm")
         nc.scalar.activation(warm[:], ident[:, 0:1], ACT.Tanh)
-        nc.vector.tensor_copy(tabs[0:16, :].bitcast(I32), tabs_in[:])
+        nc.vector.tensor_copy(tabs[0:BLOCKS, :].bitcast(I32), tabs_in[:])
 
         nc.scalar.copy(grow[0:PACK, :], gain_in[:])
         gps = psum.tile([P, HALF], F32, name="gps", tag="spare0")
         for b in range(PASSES):
             nc.tensor.transpose(gps[:, P * b : P * (b + 1)], grow[:, P * b : P * (b + 1)], ident[:])
         gcol = keep.tile([P, TILES], F32, name="gcol")
-        gpos = keep.tile([P, TILES], F32, name="gpos")
+        gtwice = keep.tile([P, TILES], F32, name="gtwice")
         gsign = keep.tile([P, TILES], F32, name="gsign")
-        nc.scalar.copy(gcol[:].rearrange("p (b t) -> p b t", t=PACK), gps[:, 0 : PASSES * P].rearrange("p (b c) -> p b c", b=PASSES)[:, :, 0:PACK])
-        nc.gpsimd.tensor_scalar(gpos[:], gcol[:], 0.0, 2.0, ALU.is_ge, ALU.mult)
-        nc.gpsimd.tensor_scalar(gsign[:], gpos[:], 1.0, -1.0, ALU.mult, ALU.add)
+        nc.scalar.copy(
+            gcol[:].rearrange("p (b t) -> p b t", t=PACK),
+            gps[:, 0 : PASSES * P].rearrange("p (b c) -> p b c", b=PASSES)[:, :, 0:PACK],
+        )
+        nc.gpsimd.tensor_scalar(gtwice[:], gcol[:], 0.0, 2.0, ALU.is_ge, ALU.mult)
+        nc.gpsimd.tensor_scalar(gsign[:], gtwice[:], 1.0, -1.0, ALU.mult, ALU.add)
+
         vw = [keep.tile([P, HALF], U32, name="vw%d" % hf, align_bytes=64) for hf in range(2)]
         vsg = keep.tile([P, S], U8, name="vsg", tag="w3", align_bytes=64)
-        rows = keep.tile([16, (S + H) // 4], I32, name="rows", tag="rows", align_bytes=64)
+        rows = keep.tile([BLOCKS, (S + H) // 4], I32, name="rows", tag="rows", align_bytes=64)
         planes = keep.tile([P, S + H], U8, name="planes", align_bytes=64)
         w4c = keep.tile([P, 2 * H], U8, name="w4c", align_bytes=64)
         nc.vector.tensor_copy(
-            rows[:, S // 4 :].rearrange("p (b t q i) -> p b t q i", b=PASSES, t=PACK, i=2),
-            w4sraw[:].rearrange("p (b q t i) -> p b t q i", b=PASSES, t=PACK, i=2),
+            rows[:, S // 4 :].rearrange("p (b t q i) -> p b t q i", b=PASSES, t=PACK, i=RUN // 4),
+            w4sraw[:].rearrange("p (b q t i) -> p b t q i", b=PASSES, t=PACK, i=RUN // 4),
         )
         nc.vector.tensor_copy(vsg[:], tabs[:].indirect(offs_t[:]))
         nc.vector.tensor_copy(
-            w4c[:].bitcast(I32).rearrange("p (b t q i) -> p b t q i", b=PASSES, t=PACK, i=4),
-            w4raw[:].bitcast(I32).rearrange("p (b q t i) -> p b t q i", b=PASSES, t=PACK, i=4),
+            w4c[:].bitcast(I32).rearrange("p (b t q i) -> p b t q i", b=PASSES, t=PACK, i=RUN // 2),
+            w4raw[:].bitcast(I32).rearrange("p (b q t i) -> p b t q i", b=PASSES, t=PACK, i=RUN // 2),
         )
-        nc.vector.tensor_copy(rows[:, 0 : S // 4], vsg[0:16, :].bitcast(I32))
-        for q in range(4):
-            nc.sync.dma_start(planes[32 * q : 32 * q + 4, :].bitcast(I32), rows[4 * q : 4 * q + 4, :])
-        load_w("w3", 0)
+        nc.vector.tensor_copy(rows[:, 0 : S // 4], vsg[0:BLOCKS, :].bitcast(I32))
+        for quad in range(BLOCKS // 4):
+            nc.sync.dma_start(planes[32 * quad : 32 * quad + 4, :].bitcast(I32), rows[4 * quad : 4 * quad + 4, :])
+        load_w("w3", 0, "w3")
         rv = keep.tile([P, NP], F32, name="rv", tag="rows", align_bytes=64)
         nc.sync.dma_start(rv[:], rowv.partition_broadcast(P))
 
-        groups = [[("w1", u) for u in range(PACK)], [("w3", 0)], [("w3", 1)], [("w3", 2), ("w3", 3)]]
+        groups = []
+        for name in ("w1", "w3"):
+            groups.extend([[(name, 0)], [(name, 1)], [(name, 2), (name, 3)]])
         groups.extend([("w3", u), ("w1", u)] for u in range(PACK, TILES))
-        wg = [keep.tile([P, 512 * len(g)], BF16, name="wg%d" % n, align_bytes=64) for n, g in enumerate(groups)]
+        wg = [keep.tile([P, PASS * len(g)], BF16, name="wg%d" % n, align_bytes=64) for n, g in enumerate(groups)]
         wcs = [keep.tile([P, P * len(g)], U32, name="wc%d" % n, align_bytes=64) for n, g in enumerate(groups)]
         wss = [keep.tile([P, P * len(g)], U8, name="ws%d" % n, align_bytes=64) for n, g in enumerate(groups)]
         place = {key: (n, a) for n, g in enumerate(groups) for a, key in enumerate(g)}
 
+        def copy_on(on_vector, dst, src):
+            if on_vector:
+                nc.vector.tensor_copy(dst, src)
+            else:
+                nc.scalar.copy(dst, src)
+
         def cast_group(n, on_vector=False):
             for a, (name, u) in enumerate(groups[n]):
                 b, t = divmod(u, PACK)
-                src = wraw[name, b][:].rearrange("p j (q t c i) -> p t q c j i", t=PACK, c=2, i=4)[:, t]
-                dst = wg[n][:, 512 * a : 512 * (a + 1)].rearrange("p (q c i j) -> p q c j i", c=2, i=4, j=PACK)
-                if on_vector:
-                    nc.vector.tensor_copy(dst, src)
-                else:
-                    nc.scalar.copy(dst, src)
+                src = wraw[name, b][:].rearrange("p j (q t c d) -> p t q c j d", t=PACK, c=RUN // 4, d=4)[:, t]
+                dst = wg[n][:, PASS * a : PASS * (a + 1)].rearrange("p (q c d j) -> p q c j d", c=RUN // 4, d=4, j=PACK)
+                copy_on(on_vector, dst, src)
 
         def quant_group(n):
             nc.vector.quantize_mx(out=wcs[n][:].bitcast(FP8X4), scales=wss[n][:], in_=wg[n][:])
 
-        cast_group(0)
-        quant_group(0)
+        for hf in range(2):
+            nc.vector.tensor_copy(vw[hf][:], tabw[:].bitcast(U32).indirect(offs_t[:, HALF // 16 * hf : HALF // 16 * (hf + 1)]))
+        load_w("w1", 1, "table")
 
-        nc.vector.tensor_copy(vw[0][:], tabw[:].bitcast(U32).indirect(offs_t[:, 0:32]))
-        nc.vector.tensor_copy(vw[1][:], tabw[:].bitcast(U32).indirect(offs_t[:, 32:64]))
-        load_w("w1", 1)
-
-        def mm(u, hf, kind):
+        def product_bank(u, hf, kind):
             if kind == "rb":
                 lhs = w4c[:, 2 * P * u : 2 * P * (u + 1)].bitcast(FP4X4)
                 lsc = planes[:, S + P * u : S + P * (u + 1)]
@@ -137,17 +148,27 @@ def tile_list_lease_conflict_desk_kernel(
                 n, a = place["w3" if kind == "st" else "w1", u]
                 lhs = wcs[n][:, P * a : P * (a + 1)].bitcast(FP8X4)
                 lsc = wss[n][:, P * a : P * (a + 1)]
-            turn = (u + {"st": 0, "ra": 2, "rb": 1}[kind]) % 3
-            bank = psum.tile([P, HALF], F32, name=kind, tag="spare%d" % hf if (u, kind) == (1, "ra") else "turn%d%d" % (turn, hf))
-            nc.tensor.matmul_mx(out=bank[:], lhsT=lhs, lhsT_scale=lsc, rhs=vw[hf][:].bitcast(FP8X4), rhs_scale=planes[:, HALF * hf : HALF * (hf + 1)], start=True, stop=True)
+            turn = (u - ("st", "ra", "rb").index(kind)) % 3
+            tag = "spare%d" % hf if (u, kind) == (1, "ra") else "turn%d%d" % (turn, hf)
+            bank = psum.tile([P, HALF], F32, name=kind, tag=tag)
+            nc.tensor.matmul_mx(
+                out=bank[:],
+                lhsT=lhs,
+                lhsT_scale=lsc,
+                rhs=vw[hf][:].bitcast(FP8X4),
+                rhs_scale=planes[:, HALF * hf : HALF * (hf + 1)],
+                start=True,
+                stop=True,
+            )
             return bank
 
         x1p = [keep.tile([P, PACK, NP], F32, name="x1p%d" % b) for b in range(PASSES)]
         g2p = [keep.tile([P, PACK, NP], F32, name="g2p%d" % b) for b in range(PASSES)]
         x2p = [keep.tile([P, PACK, NP], BF16, name="x2p%d" % b) for b in range(PASSES)]
+        picked = {"x1": x1p, "x2": x2p}
         th = {}
         ra = {}
-        mx = {}
+        larger_of = {}
         h = {}
 
         def rb_place(u, hf):
@@ -157,21 +178,21 @@ def tile_list_lease_conflict_desk_kernel(
         def first_stage(u):
             th[u] = ring.tile([P, S], F32, name="th", tag="th")
             for hf in range(2):
-                st = mm(u, hf, "st")
+                st = product_bank(u, hf, "st")
                 nc.scalar.activation(th[u][:, HALF * hf : HALF * (hf + 1)], st[:], ACT.Tanh, scale=gsign[:, u : u + 1])
             for hf in range(2):
-                rb = mm(u, hf, "rb")
+                rb = product_bank(u, hf, "rb")
                 nc.scalar.copy(rb_place(u, hf), rb[:])
-                ra[u, hf] = mm(u, hf, "ra")
+                ra[u, hf] = product_bank(u, hf, "ra")
 
         def larger(u):
-            mx[u] = ring.tile([P, S], F32, name="mx", tag="mx")
+            larger_of[u] = ring.tile([P, S], F32, name="mx", tag="mx")
             for hf in range(2):
-                nc.vector.tensor_tensor(mx[u][:, HALF * hf : HALF * (hf + 1)], ra[u, hf][:], rb_place(u, hf), ALU.max)
+                nc.vector.tensor_tensor(larger_of[u][:, HALF * hf : HALF * (hf + 1)], ra[u, hf][:], rb_place(u, hf), ALU.max)
 
-        def product(u):
+        def features(u):
             h[u] = ring.tile([P, S], F32, name="h", tag="h")
-            nc.vector.tensor_tensor(h[u][:], mx[u][:], th[u][:], ALU.mult)
+            nc.vector.tensor_tensor(h[u][:], larger_of[u][:], th[u][:], ALU.mult)
 
         def pick1(u, lo=0, hi=NP):
             b, t = divmod(u, PACK)
@@ -191,76 +212,71 @@ def tile_list_lease_conflict_desk_kernel(
                 xc[name, b] = keep.tile([P, NP], U32, name="%sc%d" % (name, b), align_bytes=64)
                 xs[name, b] = keep.tile([P, NP], U8, name="%ss%d" % (name, b), align_bytes=64)
 
-        def weave(name, b, lo, hi, on_vector=False):
-            src = {"x1": x1p, "x2": x2p}[name][b][:, :, lo:hi].rearrange("p t (c i) -> p c t i", i=4)
-            dst = xg[name, b][:, PACK * lo : PACK * hi].rearrange("p (c i t) -> p c t i", i=4, t=PACK)
-            if on_vector:
-                nc.vector.tensor_copy(dst, src)
-            else:
+        def weave_first_pass(name):
+            for lo in range(0, NP, P):
+                src = picked[name][0][:, :, lo : lo + P].rearrange("p t (c d) -> p c t d", d=4)
+                dst = xg[name, 0][:, PACK * lo : PACK * (lo + P)].rearrange("p (c d t) -> p c t d", d=4, t=PACK)
                 nc.scalar.copy(dst, src)
 
-        def weave_pair(name, t, lo, hi, on_vector=False):
-            src = {"x1": x1p, "x2": x2p}[name][1][:, t : t + 2, lo:hi].rearrange("p t c -> p c t")
-            dst = xg[name, 1][:, PACK * lo : PACK * hi].rearrange("p (c t) -> p c t", t=PACK)[:, :, t : t + 2]
-            if on_vector:
-                nc.vector.tensor_copy(dst, src)
-            else:
-                nc.scalar.copy(dst, src)
+        def weave_pair(name, t, lo, on_vector=False):
+            src = picked[name][1][:, t : t + 2, lo : lo + MID].rearrange("p t c -> p c t")
+            dst = xg[name, 1][:, PACK * lo : PACK * (lo + MID)].rearrange("p (c t) -> p c t", t=PACK)[:, :, t : t + 2]
+            copy_on(on_vector, dst, src)
 
         def quant_x(name, b, lo=0, hi=NP):
             nc.vector.quantize_mx(
                 out=xc[name, b][:, lo:hi].bitcast(FP8X4), scales=xs[name, b][:, lo:hi], in_=xg[name, b][:, PACK * lo : PACK * hi]
             )
 
-        cast_group(1, True)
-        cast_group(2, True)
-        ct = keep.tile([P, PACK, NP], F32, name="ct", tag="w1", align_bytes=64)
+        for name in ("w1", "w3"):
+            for u in range(2):
+                cast_group(place[name, u][0], True)
+            for u in range(2):
+                quant_group(place[name, u][0])
+        cast_group(place["w1", 2][0])
+        quant_group(place["w1", 2][0])
+        ct = keep.tile([P, OUT_TILES, NP], F32, name="ct", tag="w1", align_bytes=64)
         nc.sync.dma_start(ct[:], ctype.rearrange("(a p) j -> p a j", p=P))
-        quant_group(1)
-        quant_group(2)
         first_stage(0)
         for u in range(TILES):
-            ahead = place.get(("w3", u + 2), (None, None))
+            ahead = [n for n, g in enumerate(groups) if g[0] == ("w3", u + 2)]
             larger(u)
             if u + 1 < TILES:
                 first_stage(u + 1)
-            if ahead[1] is not None and u != 1:
-                cast_group(ahead[0], u == 0)
+            for n in ahead:
+                cast_group(n)
             if u == 0:
-                load_w("w3", 1)
+                load_w("w3", 1, "w3")
             if u > 0:
                 pick2(u - 1)
-            product(u)
+            features(u)
             if u > 0:
                 pick1(u - 1)
-            if ahead[1] is not None and u != 1:
-                quant_group(ahead[0])
+            for n in ahead:
+                quant_group(n)
             if u in (PACK, PACK + 1):
-                name = "x2" if u == PACK else "x1"
-                for lo in range(0, NP, P):
-                    weave(name, 0, lo, lo + P)
+                weave_first_pass(("x2", "x1")[u - PACK])
             if u == PACK + 2:
                 for name in ("x2", "x1"):
-                    for lo in (0, NP // 2):
-                        weave_pair(name, 0, lo, lo + NP // 2)
+                    for lo in (0, MID):
+                        weave_pair(name, 0, lo)
             if u in (PACK + 2, PACK + 3):
-                quant_x("x2" if u == PACK + 2 else "x1", 0)
+                quant_x(("x2", "x1")[u - PACK - 2], 0)
         last = TILES - 1
-        mid = NP // 2
-        for lo in (0, mid):
-            pick2(last, lo, lo + mid)
-            weave_pair("x2", 2, lo, lo + mid)
-        for lo in (0, mid):
-            pick1(last, lo, lo + mid)
-        for lo in (0, mid):
-            weave_pair("x1", 2, lo, lo + mid, True)
+        for lo in (0, MID):
+            pick2(last, lo, lo + MID)
+            weave_pair("x2", 2, lo)
+        for lo in (0, MID):
+            pick1(last, lo, lo + MID)
+        for lo in (0, MID):
+            weave_pair("x1", 2, lo, True)
         for name in ("x1", "x2"):
-            for lo in (0, mid):
-                quant_x(name, 1, lo, lo + mid)
+            for lo in (0, MID):
+                quant_x(name, 1, lo, lo + MID)
 
         es = []
-        for a in range(PACK):
-            e = psum.tile([P, NP], F32, name="e", tag="turn%d%d" % ((TILES - 1 + a // 2) % 3, a % 2))
+        for a in range(OUT_TILES):
+            e = psum.tile([P, NP], F32, name="e", tag="turn%d%d" % ((last + a // 2) % 3, a % 2))
             for b in range(PASSES):
                 nc.tensor.matmul_mx(
                     out=e[:],
@@ -272,13 +288,13 @@ def tile_list_lease_conflict_desk_kernel(
                     stop=(b == PASSES - 1),
                 )
             es.append(e)
-        scaled = [keep.tile([P, NP], F32, name="scaled%d" % a) for a in range(PACK)]
-        res = [keep.tile([P, NP], F32, name="res%d" % a) for a in range(PACK)]
-        for a in range(PACK):
+        scaled = [keep.tile([P, NP], F32, name="scaled%d" % a) for a in range(OUT_TILES)]
+        res = [keep.tile([P, NP], F32, name="res%d" % a) for a in range(OUT_TILES)]
+        for a in range(OUT_TILES):
             nc.vector.tensor_tensor(scaled[a][:], es[a][:], ct[:, a, :], ALU.mult)
-        for a in range(PACK):
+        for a in range(OUT_TILES):
             adder = nc.gpsimd if a == 0 else nc.vector
-            step = mid if a == PACK - 1 else NP
+            step = MID if a == OUT_TILES - 1 else NP
             for lo in range(0, NP, step):
                 adder.tensor_tensor(res[a][:, lo : lo + step], scaled[a][:, lo : lo + step], rv[:, lo : lo + step], ALU.add)
                 nc.sync.dma_start(out[P * a : P * (a + 1), lo : lo + step], res[a][:, lo : lo + step])

from contextlib import ExitStack

import concourse.mybir as mybir
from concourse.masks import make_identity

K, H, T, S, NP = 512, 1024, 4096, 1024, 512
FLOPS = 2 * 3 * K * H * S + 2 * H * NP * NP

F32 = mybir.dt.float32
BF16 = mybir.dt.bfloat16
I32 = mybir.dt.int32
U32 = mybir.dt.uint32
U16 = mybir.dt.uint16
U8 = mybir.dt.uint8
FP8X4 = mybir.dt.float8_e4m3fn_x4
FP4X4 = mybir.dt.float4_e2m1fn_x4
ACT = mybir.ActivationFunctionType
ALU = mybir.AluOpType

P = 128
PACK = 4
PASS = P * PACK
BLOCKS = PASS // 32
RUN = 8
HALF = 512
PASSES = H // PASS
TILES = PASSES * PACK
OUT_TILES = NP // P
MID = NP // 2


def tile_list_lease_conflict_desk_kernel(
    tc, tab_words, tab_scales, offs, pos1, pos2, w1, w4_words, w4_scales, w3, gain, ctype, rowv, out
):
    nc = tc.nc
    with ExitStack() as ctx:
        keep = ctx.enter_context(tc.tile_pool(name="keep", bufs=1))
        ring = ctx.enter_context(tc.tile_pool(name="ring", bufs=2))
        psum = ctx.enter_context(tc.psum_pool(name="psum", bufs=1))

        offs_t = keep.tile([P, S // 16], U16, name="offs_t")
        pos1_t = keep.tile([P, NP // 16], U16, name="pos1_t")
        pos2_t = keep.tile([P, NP // 16], U16, name="pos2_t")
        tabw = keep.tile([P, T], I32, name="tabw", tag="table", align_bytes=64)
        tabs_in = keep.tile([BLOCKS, T // 4], I32, name="tabs_in", align_bytes=64)
        tabs = keep.tile([P, T], U8, name="tabs", align_bytes=64)
        w4raw = keep.tile([P, 2 * H], U8, name="w4raw", align_bytes=64)
        w4sraw = keep.tile([BLOCKS, H // 4], I32, name="w4sraw", align_bytes=64)
        gain_in = keep.tile([PACK, PASSES * P], F32, name="gain_in")
        grow = keep.tile([P, PASSES * P], F32, name="grow")
        ident = keep.tile([P, P], F32, name="ident")
        wsrc = {"w3": w3, "w1": w1}
        wraw = {}

        def load_w(name, b, tag):
            wraw[name, b] = keep.tile([P, PACK, PASS], F32, name="%sraw%d" % (name, b), tag=tag, align_bytes=64)
            nc.sync.dma_start(wraw[name, b][:], wsrc[name][:, PASS * b : PASS * (b + 1)].rearrange("(p j) c -> p j c", j=PACK))

        nc.sync.dma_start(tabs_in[:], tab_scales[0].bitcast(I32))
        nc.sync.dma_start(offs_t[:], offs)
        nc.sync.dma_start(pos2_t[:], pos2)
        nc.sync.dma_start(w4sraw[:], w4_scales[0].bitcast(I32))
        nc.sync.dma_start(
            gain_in[:].rearrange("t (g i) -> t g i", i=RUN),
            gain.rearrange("(g t i) -> t g i", t=PACK, i=RUN),
        )
        nc.sync.dma_start(w4raw[:].bitcast(I32), w4_words[0].bitcast(I32))
        nc.sync.dma_start(tabw[:], tab_words[0].rearrange("p t i -> p (t i)").bitcast(I32))
        load_w("w1", 0, "w1")
        nc.sync.dma_start(pos1_t[:], pos1)

        nc.gpsimd.memset(grow[:], 0.0)
        make_identity(nc, ident[:])
        nc.vector.memset(tabs[:].bitcast(I32), 0)
        warm = keep.tile([P, 1], F32, name="warm")
        nc.scalar.activation(warm[:], ident[:, 0:1], ACT.Tanh)
        nc.vector.tensor_copy(tabs[0:BLOCKS, :].bitcast(I32), tabs_in[:])

        nc.scalar.copy(grow[0:PACK, :], gain_in[:])
        gps = psum.tile([P, HALF], F32, name="gps", tag="spare0")
        for b in range(PASSES):
            nc.tensor.transpose(gps[:, P * b : P * (b + 1)], grow[:, P * b : P * (b + 1)], ident[:])
        gcol = keep.tile([P, TILES], F32, name="gcol")
        gtwice = keep.tile([P, TILES], F32, name="gtwice")
        gsign = keep.tile([P, TILES], F32, name="gsign")
        nc.scalar.copy(
            gcol[:].rearrange("p (b t) -> p b t", t=PACK),
            gps[:, 0 : PASSES * P].rearrange("p (b c) -> p b c", b=PASSES)[:, :, 0:PACK],
        )
        nc.gpsimd.tensor_scalar(gtwice[:], gcol[:], 0.0, 2.0, ALU.is_ge, ALU.mult)
        nc.gpsimd.tensor_scalar(gsign[:], gtwice[:], 1.0, -1.0, ALU.mult, ALU.add)

        vw = [keep.tile([P, HALF], U32, name="vw%d" % hf, align_bytes=64) for hf in range(2)]
        vsg = keep.tile([P, S], U8, name="vsg", tag="w3", align_bytes=64)
        rows = keep.tile([BLOCKS, (S + H) // 4], I32, name="rows", tag="rows", align_bytes=64)
        planes = keep.tile([P, S + H], U8, name="planes", align_bytes=64)
        w4c = keep.tile([P, 2 * H], U8, name="w4c", align_bytes=64)
        nc.vector.tensor_copy(
            rows[:, S // 4 :].rearrange("p (b t q i) -> p b t q i", b=PASSES, t=PACK, i=RUN // 4),
            w4sraw[:].rearrange("p (b q t i) -> p b t q i", b=PASSES, t=PACK, i=RUN // 4),
        )
        nc.vector.tensor_copy(vsg[:], tabs[:].indirect(offs_t[:]))
        nc.vector.tensor_copy(
            w4c[:].bitcast(I32).rearrange("p (b t q i) -> p b t q i", b=PASSES, t=PACK, i=RUN // 2),
            w4raw[:].bitcast(I32).rearrange("p (b q t i) -> p b t q i", b=PASSES, t=PACK, i=RUN // 2),
        )
        nc.vector.tensor_copy(rows[:, 0 : S // 4], vsg[0:BLOCKS, :].bitcast(I32))
        for quad in range(BLOCKS // 4):
            nc.sync.dma_start(planes[32 * quad : 32 * quad + 4, :].bitcast(I32), rows[4 * quad : 4 * quad + 4, :])
        load_w("w3", 0, "w3")
        rv = keep.tile([P, NP], F32, name="rv", tag="rows", align_bytes=64)
        nc.sync.dma_start(rv[:], rowv.partition_broadcast(P))

        groups = []
        for name in ("w1", "w3"):
            groups.extend([[(name, 0)], [(name, 1)], [(name, 2), (name, 3)]])
        groups.extend([("w3", u), ("w1", u)] for u in range(PACK, TILES))
        wg = [keep.tile([P, PASS * len(g)], BF16, name="wg%d" % n, align_bytes=64) for n, g in enumerate(groups)]
        wcs = [keep.tile([P, P * len(g)], U32, name="wc%d" % n, align_bytes=64) for n, g in enumerate(groups)]
        wss = [keep.tile([P, P * len(g)], U8, name="ws%d" % n, align_bytes=64) for n, g in enumerate(groups)]
        place = {key: (n, a) for n, g in enumerate(groups) for a, key in enumerate(g)}

        def copy_on(on_vector, dst, src):
            if on_vector:
                nc.vector.tensor_copy(dst, src)
            else:
                nc.scalar.copy(dst, src)

        def cast_group(n, on_vector=False):
            for a, (name, u) in enumerate(groups[n]):
                b, t = divmod(u, PACK)
                src = wraw[name, b][:].rearrange("p j (q t c d) -> p t q c j d", t=PACK, c=RUN // 4, d=4)[:, t]
                dst = wg[n][:, PASS * a : PASS * (a + 1)].rearrange("p (q c d j) -> p q c j d", c=RUN // 4, d=4, j=PACK)
                copy_on(on_vector, dst, src)

        def quant_group(n):
            nc.vector.quantize_mx(out=wcs[n][:].bitcast(FP8X4), scales=wss[n][:], in_=wg[n][:])

        for hf in range(2):
            nc.vector.tensor_copy(vw[hf][:], tabw[:].bitcast(U32).indirect(offs_t[:, HALF // 16 * hf : HALF // 16 * (hf + 1)]))
        load_w("w1", 1, "table")

        def product_bank(u, hf, kind):
            if kind == "rb":
                lhs = w4c[:, 2 * P * u : 2 * P * (u + 1)].bitcast(FP4X4)
                lsc = planes[:, S + P * u : S + P * (u + 1)]
            else:
                n, a = place["w3" if kind == "st" else "w1", u]
                lhs = wcs[n][:, P * a : P * (a + 1)].bitcast(FP8X4)
                lsc = wss[n][:, P * a : P * (a + 1)]
            turn = (u - ("st", "ra", "rb").index(kind)) % 3
            tag = "spare%d" % hf if (u, kind) == (1, "ra") else "turn%d%d" % (turn, hf)
            bank = psum.tile([P, HALF], F32, name=kind, tag=tag)
            nc.tensor.matmul_mx(
                out=bank[:],
                lhsT=lhs,
                lhsT_scale=lsc,
                rhs=vw[hf][:].bitcast(FP8X4),
                rhs_scale=planes[:, HALF * hf : HALF * (hf + 1)],
                start=True,
                stop=True,
            )
            return bank

        x1p = [keep.tile([P, PACK, NP], F32, name="x1p%d" % b) for b in range(PASSES)]
        g2p = [keep.tile([P, PACK, NP], F32, name="g2p%d" % b) for b in range(PASSES)]
        x2p = [keep.tile([P, PACK, NP], BF16, name="x2p%d" % b) for b in range(PASSES)]
        picked = {"x1": x1p, "x2": x2p}
        th = {}
        ra = {}
        larger_of = {}
        h = {}

        def rb_place(u, hf):
            b, t = divmod(max(u - 1, 0), PACK)
            return (g2p, x1p)[hf][b][:, t, :]

        def first_stage(u):
            th[u] = ring.tile([P, S], F32, name="th", tag="th")
            for hf in range(2):
                st = product_bank(u, hf, "st")
                nc.scalar.activation(th[u][:, HALF * hf : HALF * (hf + 1)], st[:], ACT.Tanh, scale=gsign[:, u : u + 1])
            for hf in range(2):
                rb = product_bank(u, hf, "rb")
                nc.scalar.copy(rb_place(u, hf), rb[:])
                ra[u, hf] = product_bank(u, hf, "ra")

        def larger(u):
            larger_of[u] = ring.tile([P, S], F32, name="mx", tag="mx")
            for hf in range(2):
                nc.vector.tensor_tensor(larger_of[u][:, HALF * hf : HALF * (hf + 1)], ra[u, hf][:], rb_place(u, hf), ALU.max)

        def features(u):
            h[u] = ring.tile([P, S], F32, name="h", tag="h")
            nc.vector.tensor_tensor(h[u][:], larger_of[u][:], th[u][:], ALU.mult)

        def pick1(u, lo=0, hi=NP):
            b, t = divmod(u, PACK)
            nc.vector.tensor_copy(x1p[b][:, t, lo:hi], h[u][:].indirect(pos1_t[:, lo // 16 : hi // 16]))

        def pick2(u, lo=0, hi=NP):
            b, t = divmod(u, PACK)
            nc.vector.tensor_copy(g2p[b][:, t, lo:hi], h[u][:].indirect(pos2_t[:, lo // 16 : hi // 16]))
            nc.scalar.activation(x2p[b][:, t, lo:hi], g2p[b][:, t, lo:hi], ACT.Abs, scale=gcol[:, u : u + 1])

        xg = {}
        xc = {}
        xs = {}
        for name in ("x1", "x2"):
            for b in range(PASSES):
                xg[name, b] = keep.tile([P, PACK * NP], BF16, name="%sg%d" % (name, b), align_bytes=64)
                xc[name, b] = keep.tile([P, NP], U32, name="%sc%d" % (name, b), align_bytes=64)
                xs[name, b] = keep.tile([P, NP], U8, name="%ss%d" % (name, b), align_bytes=64)

        def weave_first_pass(name):
            for lo in range(0, NP, P):
                src = picked[name][0][:, :, lo : lo + P].rearrange("p t (c d) -> p c t d", d=4)
                dst = xg[name, 0][:, PACK * lo : PACK * (lo + P)].rearrange("p (c d t) -> p c t d", d=4, t=PACK)
                nc.scalar.copy(dst, src)

        def weave_pair(name, t, lo, on_vector=False):
            src = picked[name][1][:, t : t + 2, lo : lo + MID].rearrange("p t c -> p c t")
            dst = xg[name, 1][:, PACK * lo : PACK * (lo + MID)].rearrange("p (c t) -> p c t", t=PACK)[:, :, t : t + 2]
            copy_on(on_vector, dst, src)

        def quant_x(name, b, lo=0, hi=NP):
            nc.vector.quantize_mx(
                out=xc[name, b][:, lo:hi].bitcast(FP8X4), scales=xs[name, b][:, lo:hi], in_=xg[name, b][:, PACK * lo : PACK * hi]
            )

        for name in ("w1", "w3"):
            for u in range(2):
                cast_group(place[name, u][0], True)
            for u in range(2):
                quant_group(place[name, u][0])
        cast_group(place["w1", 2][0])
        quant_group(place["w1", 2][0])
        ct = keep.tile([P, OUT_TILES, NP], F32, name="ct", tag="w1", align_bytes=64)
        nc.sync.dma_start(ct[:], ctype.rearrange("(a p) j -> p a j", p=P))
        first_stage(0)
        for u in range(TILES):
            ahead = [n for n, g in enumerate(groups) if g[0] == ("w3", u + 2)]
            larger(u)
            if u + 1 < TILES:
                first_stage(u + 1)
            for n in ahead:
                cast_group(n)
            if u == 0:
                load_w("w3", 1, "w3")
            if u > 0:
                pick2(u - 1)
            features(u)
            if u > 0:
                pick1(u - 1)
            for n in ahead:
                quant_group(n)
            if u in (PACK, PACK + 1):
                weave_first_pass(("x2", "x1")[u - PACK])
            if u == PACK + 2:
                for name in ("x2", "x1"):
                    for lo in (0, MID):
                        weave_pair(name, 0, lo)
            if u in (PACK + 2, PACK + 3):
                quant_x(("x2", "x1")[u - PACK - 2], 0)
        last = TILES - 1
        for lo in (0, MID):
            pick2(last, lo, lo + MID)
            weave_pair("x2", 2, lo)
        for lo in (0, MID):
            pick1(last, lo, lo + MID)
        for lo in (0, MID):
            weave_pair("x1", 2, lo, True)
        for name in ("x1", "x2"):
            for lo in (0, MID):
                quant_x(name, 1, lo, lo + MID)

        es = []
        for a in range(OUT_TILES):
            e = psum.tile([P, NP], F32, name="e", tag="turn%d%d" % ((last + a // 2) % 3, a % 2))
            for b in range(PASSES):
                nc.tensor.matmul_mx(
                    out=e[:],
                    lhsT=xc["x1", b][:, P * a : P * (a + 1)].bitcast(FP8X4),
                    lhsT_scale=xs["x1", b][:, P * a : P * (a + 1)],
                    rhs=xc["x2", b][:].bitcast(FP8X4),
                    rhs_scale=xs["x2", b][:],
                    start=(b == 0),
                    stop=(b == PASSES - 1),
                )
            es.append(e)
        scaled = [keep.tile([P, NP], F32, name="scaled%d" % a) for a in range(OUT_TILES)]
        res = [keep.tile([P, NP], F32, name="res%d" % a) for a in range(OUT_TILES)]
        for a in range(OUT_TILES):
            nc.vector.tensor_tensor(scaled[a][:], es[a][:], ct[:, a, :], ALU.mult)
        for a in range(OUT_TILES):
            adder = nc.gpsimd if a == 0 else nc.vector
            step = MID if a == OUT_TILES - 1 else NP
            for lo in range(0, NP, step):
                adder.tensor_tensor(res[a][:, lo : lo + step], scaled[a][:, lo : lo + step], rv[:, lo : lo + step], ALU.add)
                nc.sync.dma_start(out[P * a : P * (a + 1), lo : lo + step], res[a][:, lo : lo + step])
